import numpy as np, ml_dtypes
CORES = [125,127,253,255,381,383,509,511]
N = 8
WB, KB, QP = 1, 4, 64
def setup_inputs(rng):
    return {"q": rng.standard_normal((N, 128, QP), dtype=np.float32).astype(ml_dtypes.bfloat16), "k": rng.standard_normal((N, 128, KB * 128), dtype=np.float32).astype(ml_dtypes.bfloat16), "v": rng.standard_normal((N, 128, KB * 128), dtype=np.float32).astype(ml_dtypes.bfloat16)}
def setup_inputs_big(rng):
    d = setup_inputs(rng)
    for k in ("q", "k", "v"): d[k] = (d[k].astype(np.float32) * 1024.0).astype(d[k].dtype)
    return d
def setup_inputs_small(rng):
    d = setup_inputs(rng)
    for k in ("q", "k", "v"): d[k] = (d[k].astype(np.float32) * (1 / 1024.0)).astype(d[k].dtype)
    return d
def setup_inputs_apart(rng):
    d = setup_inputs(rng)
    f = (10.0 ** rng.permutation(np.linspace(-1.5, 1.5, N))).astype(np.float32).reshape(N, 1, 1)
    for k in ("q", "k", "v"): d[k] = (d[k].astype(np.float32) * f).astype(d[k].dtype)
    return d
def reference(q, k, v):
    Q, K, V = q.astype(np.float64), k.astype(np.float64), v.astype(np.float64)
    y = np.zeros((N, 128, QP))
    for r in range(N):
        for j in range(max(0, r - WB), r + 1):
            for b in range(KB):
                S = np.maximum(K[j][:, 128 * b:128 * b + 128].T @ Q[r], 0.0)
                y[r] += V[j][:, 128 * b:128 * b + 128].T @ S
    return {"y": y.astype(ml_dtypes.bfloat16 if q.dtype != np.float64 else np.float64)}

@@ -1,0 +1,145 @@
+from concourse.mybir import AluOpType
+
+P, QP, BW, KB = 128, 64, 128, 4
+ENG = 8
+ENG_HEAD = 16
+
+SCRATCH = {
+    "qd":    ("dram", [P, QP], "bfloat16"),
+    "q_sb":  ("sbuf", [P, QP], "bfloat16"),
+    "qn_sb": ("sbuf", [P, QP], "bfloat16"),
+    "k_sb":  ("sbuf", [P, KB * BW], "bfloat16"),
+    "v_sb":  ("sbuf", [P, KB * BW], "bfloat16"),
+    "kvx":   ("sbuf", [P, 2 * BW], "bfloat16"),
+    "zero":  ("sbuf", [P, (KB + 1) * QP], "bfloat16"),
+    "sn_sb": ("sbuf", [P, KB * QP], "bfloat16"),
+    "so_sb": ("sbuf", [P, (KB + 1) * QP], "bfloat16"),
+    "os_sb": ("sbuf", [P, QP], "bfloat16"),
+    "on_sb": ("sbuf", [P, QP], "bfloat16"),
+    "y_sb":  ("sbuf", [P, QP], "bfloat16"),
+    "psn0":  ("psum", [P, 512], "float32"),
+    "psn1":  ("psum", [P, 512], "float32"),
+    "psn2":  ("psum", [P, 512], "float32"),
+    "psn3":  ("psum", [P, 512], "float32"),
+    "pon":   ("psum", [P, 512], "float32"),
+    "pso":   ("psum", [P, 512], "float32"),
+    "poo":   ("psum", [P, 512], "float32"),
+}
+SEMAPHORES = ["qd", "q", "k", "v", "kx", "z", "qn", "on", "kvn", "loc",
+              "m1n0", "m1n1", "m1n2", "m1n3", "rn0", "rn1", "rn2", "rn3", "m2n", "cn",
+              "m1o", "ro", "m2o", "ydone", "st"]
+
+
+def _engines(topo, src, dst, want):
+    full, m, cnt, bit = topo.mask(src, dst), 0, 0, 1
+    while cnt < want and bit <= full:
+        if full & bit:
+            m |= bit
+            cnt += 1
+        bit <<= 1
+    return m, cnt
+
+
+def rank_program(g, core, T, topo):
+    r = T.rank_of(core)
+    if r is None:
+        return
+    cores, S = T.cores, T.sem
+    last = len(cores) - 1
+    te, ve, sy, sc = g.tensor, g.vector, g.sync, g.scalar
+    head, second = (r == 0), (r == 1)
+
+    def q_eng(i):
+        return _engines(topo, cores[i], cores[i - 1], ENG)
+
+    def o_eng(i):
+        return _engines(topo, cores[i], cores[i + 1], ENG_HEAD if i == 0 else ENG)
+
+    def blk(t, b):
+        return t[:, b * BW:(b + 1) * BW]
+
+    if head:
+        sy.dma_start(T.kvx[:, 0:BW], blk(T.k, KB - 1)).then_inc(S.kx, 16)
+        sy.dma_start(T.kvx[:, BW:2 * BW], blk(T.v, KB - 1)).then_inc(S.kx, 16)
+        w = (KB - 1) * BW
+        sy.dma_start(T.k_sb[:, 0:w], T.k[:, 0:w]).then_inc(S.k, 16)
+        sy.dma_start(T.v_sb[:, 0:w], T.v[:, 0:w]).then_inc(S.v, 16)
+    else:
+        sy.dma_start(T.qd[:], T.q[:]).then_inc(S.qd, 16)
+        sy.dma_start(T.k_sb[:], T.k[:]).then_inc(S.k, 16)
+        sy.dma_start(T.v_sb[:], T.v[:]).then_inc(S.v, 16)
+    sy.dma_start(T.q_sb[:], T.q[:]).then_inc(S.q, 16)
+
+    kept = KB - 1 if head else KB
+    nb = [(blk(T.k_sb, b), blk(T.v_sb, b)) for b in range(kept)]
+    ob = list(nb)
+    if head or second:
+        ob.append((T.kvx[:, 0:BW], T.kvx[:, BW:2 * BW]))
+
+    sent = 0
+    if head:
+        m, e = o_eng(0)
+        rid, pid = topo.addr(cores[1], core)
+        g.wait_ge(S.kx, 32)
+        g.remote_dma(T.kvx[:], T.kvx[:], S.kvn, S.loc, pid, rid, m)
+        sent += e
+    else:
+        m, e = q_eng(r)
+        rid, pid = topo.addr(cores[r - 1], core)
+        g.wait_ge(S.qd, 16)
+        g.remote_dma(T.qn_sb[:], T.qd[:], S.qn, S.loc, pid, rid, m)
+        sent += e
+    if r < last:
+        m, e = o_eng(r)
+        rid, pid = topo.addr(cores[r + 1], core)
+        g.wait_ge(S.cn, 1)
+        g.remote_dma(T.on_sb[:], T.os_sb[:], S.on, S.loc, pid, rid, m)
+        sent += e
+    g.wait_ge(S.loc, sent)
+
+    if r < last:
+        te.wait_ge(S.k, 16)
+        te.wait_ge(S.qn, q_eng(r + 1)[1])
+        for i, (kb, vb) in enumerate(nb):
+            te.matmul(T["psn%d" % i][:, 0:QP], kb, T.qn_sb[:], start=True, stop=True).then_inc(S["m1n%d" % i], 1)
+        te.wait_ge(S.v, 16)
+        for i, (kb, vb) in enumerate(nb):
+            te.wait_ge(S["rn%d" % i], 1)
+            te.matmul(T.pon[:, 0:QP], vb, T.sn_sb[:, i * QP:(i + 1) * QP],
+                      start=(i == 0), stop=(i == len(nb) - 1)).then_inc(S.m2n, 1)
+    te.wait_ge(S.k, 16)
+    te.wait_ge(S.v, 16)
+    te.wait_ge(S.q, 16)
+    if head:
+        te.wait_ge(S.kx, 32)
+    if second:
+        te.wait_ge(S.kvn, o_eng(0)[1])
+    for i, (kb, vb) in enumerate(ob):
+        te.matmul(T.pso[:, i * QP:(i + 1) * QP], kb, T.q_sb[:], start=True, stop=True).then_inc(S.m1o, 1)
+    te.wait_ge(S.ro, 1)
+    for i, (kb, vb) in enumerate(ob):
+        te.matmul(T.poo[:, 0:QP], vb, T.so_sb[:, i * QP:(i + 1) * QP],
+                  start=(i == 0), stop=(i == len(ob) - 1)).then_inc(S.m2o, 1)
+
+    ve.memset(T.zero[:], 0.0).then_inc(S.z, 1)
+    ve.wait_ge(S.z, 1)
+    if r < last:
+        for i in range(len(nb)):
+            ve.wait_ge(S["m1n%d" % i], 1)
+            ve.tensor_tensor(T.sn_sb[:, i * QP:(i + 1) * QP], T["psn%d" % i][:, 0:QP], T.zero[:, 0:QP],
+                             AluOpType.max).then_inc(S["rn%d" % i], 1)
+        ve.wait_ge(S.m2n, len(nb))
+        ve.tensor_copy(T.os_sb[:], T.pon[:, 0:QP]).then_inc(S.cn, 1)
+    wo = len(ob) * QP
+    ve.wait_ge(S.m1o, len(ob))
+    ve.tensor_tensor(T.so_sb[:, 0:wo], T.pso[:, 0:wo], T.zero[:, 0:wo], AluOpType.max).then_inc(S.ro, 1)
+    ve.wait_ge(S.m2o, len(ob))
+    if head:
+        ve.tensor_copy(T.y_sb[:], T.poo[:, 0:QP]).then_inc(S.ydone, 1)
+    else:
+        ve.wait_ge(S.on, o_eng(r - 1)[1])
+        ve.tensor_tensor(T.y_sb[:], T.poo[:, 0:QP], T.on_sb[:], AluOpType.add).then_inc(S.ydone, 1)
+
+    sc.wait_ge(S.ydone, 1)
+    sc.dma_start(T.y[:], T.y_sb[:]).then_inc(S.st, 16)
+    sc.wait_ge(S.st, 16)

@@ -6,6 +6,7 @@ ENG_HEAD = 16
 
 SCRATCH = {
     "qd":    ("dram", [P, QP], "bfloat16"),
+    "yd":    ("dram", [P, QP], "bfloat16"),
     "q_sb":  ("sbuf", [P, QP], "bfloat16"),
     "qn_sb": ("sbuf", [P, QP], "bfloat16"),
     "k_sb":  ("sbuf", [P, KB * BW], "bfloat16"),
@@ -16,6 +17,8 @@ SCRATCH = {
     "so_sb": ("sbuf", [P, (KB + 1) * QP], "bfloat16"),
     "os_sb": ("sbuf", [P, QP], "bfloat16"),
     "on_sb": ("sbuf", [P, QP], "bfloat16"),
+    "ps_sb": ("sbuf", [P, QP], "bfloat16"),
+    "pn_sb": ("sbuf", [P, QP], "bfloat16"),
     "y_sb":  ("sbuf", [P, QP], "bfloat16"),
     "psn0":  ("psum", [P, 512], "float32"),
     "psn1":  ("psum", [P, 512], "float32"),
@@ -25,7 +28,7 @@ SCRATCH = {
     "pso":   ("psum", [P, 512], "float32"),
     "poo":   ("psum", [P, 512], "float32"),
 }
-SEMAPHORES = ["qd", "q", "k", "v", "kx", "z", "qn", "on", "kvn", "loc",
+SEMAPHORES = ["qd", "q", "k", "v", "kx", "z", "qn", "on", "kvn", "loc", "pn", "pc",
               "m1n0", "m1n1", "m1n2", "m1n3", "rn0", "rn1", "rn2", "rn3", "m2n", "cn",
               "m1o", "ro", "m2o", "ydone", "st"]
 
@@ -49,6 +52,13 @@ def rank_program(g, core, T, topo):
     te, ve, sy, sc = g.tensor, g.vector, g.sync, g.scalar
     head, second = (r == 0), (r == 1)
 
+    def apart(i):
+        a, b = cores[i - 1], cores[i]
+        return (topo.host(a), topo.chip(a)) != (topo.host(b), topo.chip(b))
+
+    client = r > 0 and apart(r)
+    finisher = r < last and apart(r + 1)
+
     def q_eng(i):
         return _engines(topo, cores[i], cores[i - 1], ENG)
 
@@ -64,11 +74,15 @@ def rank_program(g, core, T, topo):
         w = (KB - 1) * BW
         sy.dma_start(T.k_sb[:, 0:w], T.k[:, 0:w]).then_inc(S.k, 16)
         sy.dma_start(T.v_sb[:, 0:w], T.v[:, 0:w]).then_inc(S.v, 16)
+        sy.dma_start(T.q_sb[:], T.q[:]).then_inc(S.q, 16)
     else:
         sy.dma_start(T.qd[:], T.q[:]).then_inc(S.qd, 16)
+        if client:
+            sy.dma_start(T.q_sb[:], T.q[:]).then_inc(S.q, 16)
         sy.dma_start(T.k_sb[:], T.k[:]).then_inc(S.k, 16)
         sy.dma_start(T.v_sb[:], T.v[:]).then_inc(S.v, 16)
-    sy.dma_start(T.q_sb[:], T.q[:]).then_inc(S.q, 16)
+        if not client:
+            sy.dma_start(T.q_sb[:], T.q[:]).then_inc(S.q, 16)
 
     kept = KB - 1 if head else KB
     nb = [(blk(T.k_sb, b), blk(T.v_sb, b)) for b in range(kept)]
@@ -89,15 +103,19 @@ def rank_program(g, core, T, topo):
         g.wait_ge(S.qd, 16)
         g.remote_dma(T.qn_sb[:], T.qd[:], S.qn, S.loc, pid, rid, m)
         sent += e
+        if client:
+            g.wait_ge(S.pc, 1)
+            g.remote_dma(T.pn_sb[:], T.ps_sb[:], S.pn, S.loc, pid, rid, m)
+            sent += e
     if r < last:
         m, e = o_eng(r)
         rid, pid = topo.addr(cores[r + 1], core)
         g.wait_ge(S.cn, 1)
-        g.remote_dma(T.on_sb[:], T.os_sb[:], S.on, S.loc, pid, rid, m)
+        g.remote_dma(T.yd[:] if finisher else T.on_sb[:], T.os_sb[:], S.on, S.loc, pid, rid, m)
         sent += e
     g.wait_ge(S.loc, sent)
 
-    if r < last:
+    def te_serve():
         te.wait_ge(S.k, 16)
         te.wait_ge(S.qn, q_eng(r + 1)[1])
         for i, (kb, vb) in enumerate(nb):
@@ -107,39 +125,67 @@ def rank_program(g, core, T, topo):
             te.wait_ge(S["rn%d" % i], 1)
             te.matmul(T.pon[:, 0:QP], vb, T.sn_sb[:, i * QP:(i + 1) * QP],
                       start=(i == 0), stop=(i == len(nb) - 1)).then_inc(S.m2n, 1)
-    te.wait_ge(S.k, 16)
-    te.wait_ge(S.v, 16)
-    te.wait_ge(S.q, 16)
-    if head:
-        te.wait_ge(S.kx, 32)
-    if second:
-        te.wait_ge(S.kvn, o_eng(0)[1])
-    for i, (kb, vb) in enumerate(ob):
-        te.matmul(T.pso[:, i * QP:(i + 1) * QP], kb, T.q_sb[:], start=True, stop=True).then_inc(S.m1o, 1)
-    te.wait_ge(S.ro, 1)
-    for i, (kb, vb) in enumerate(ob):
-        te.matmul(T.poo[:, 0:QP], vb, T.so_sb[:, i * QP:(i + 1) * QP],
-                  start=(i == 0), stop=(i == len(ob) - 1)).then_inc(S.m2o, 1)
 
-    ve.memset(T.zero[:], 0.0).then_inc(S.z, 1)
-    ve.wait_ge(S.z, 1)
+    def te_own():
+        te.wait_ge(S.k, 16)
+        te.wait_ge(S.q, 16)
+        if head:
+            te.wait_ge(S.kx, 32)
+        if second:
+            te.wait_ge(S.kvn, o_eng(0)[1])
+        for i, (kb, vb) in enumerate(ob):
+            te.matmul(T.pso[:, i * QP:(i + 1) * QP], kb, T.q_sb[:], start=True, stop=True).then_inc(S.m1o, 1)
+        te.wait_ge(S.v, 16)
+        te.wait_ge(S.ro, 1)
+        for i, (kb, vb) in enumerate(ob):
+            te.matmul(T.poo[:, 0:QP], vb, T.so_sb[:, i * QP:(i + 1) * QP],
+                      start=(i == 0), stop=(i == len(ob) - 1)).then_inc(S.m2o, 1)
+
+    if client:
+        te_own()
     if r < last:
+        te_serve()
+    if not client:
+        te_own()
+
+    def ve_serve():
         for i in range(len(nb)):
             ve.wait_ge(S["m1n%d" % i], 1)
             ve.tensor_tensor(T.sn_sb[:, i * QP:(i + 1) * QP], T["psn%d" % i][:, 0:QP], T.zero[:, 0:QP],
                              AluOpType.max).then_inc(S["rn%d" % i], 1)
         ve.wait_ge(S.m2n, len(nb))
-        ve.tensor_copy(T.os_sb[:], T.pon[:, 0:QP]).then_inc(S.cn, 1)
-    wo = len(ob) * QP
-    ve.wait_ge(S.m1o, len(ob))
-    ve.tensor_tensor(T.so_sb[:, 0:wo], T.pso[:, 0:wo], T.zero[:, 0:wo], AluOpType.max).then_inc(S.ro, 1)
-    ve.wait_ge(S.m2o, len(ob))
-    if head:
-        ve.tensor_copy(T.y_sb[:], T.poo[:, 0:QP]).then_inc(S.ydone, 1)
-    else:
-        ve.wait_ge(S.on, o_eng(r - 1)[1])
-        ve.tensor_tensor(T.y_sb[:], T.poo[:, 0:QP], T.on_sb[:], AluOpType.add).then_inc(S.ydone, 1)
+        if finisher:
+            ve.wait_ge(S.pn, q_eng(r + 1)[1])
+            ve.tensor_tensor(T.os_sb[:], T.pon[:, 0:QP], T.pn_sb[:], AluOpType.add).then_inc(S.cn, 1)
+        else:
+            ve.tensor_copy(T.os_sb[:], T.pon[:, 0:QP]).then_inc(S.cn, 1)
 
-    sc.wait_ge(S.ydone, 1)
-    sc.dma_start(T.y[:], T.y_sb[:]).then_inc(S.st, 16)
+    def ve_own():
+        wo = len(ob) * QP
+        ve.wait_ge(S.m1o, len(ob))
+        ve.tensor_tensor(T.so_sb[:, 0:wo], T.pso[:, 0:wo], T.zero[:, 0:wo], AluOpType.max).then_inc(S.ro, 1)
+        ve.wait_ge(S.m2o, len(ob))
+        if client:
+            ve.tensor_copy(T.ps_sb[:], T.poo[:, 0:QP]).then_inc(S.pc, 1)
+        elif head:
+            ve.tensor_copy(T.y_sb[:], T.poo[:, 0:QP]).then_inc(S.ydone, 1)
+        else:
+            ve.wait_ge(S.on, o_eng(r - 1)[1])
+            ve.tensor_tensor(T.y_sb[:], T.poo[:, 0:QP], T.on_sb[:], AluOpType.add).then_inc(S.ydone, 1)
+
+    ve.memset(T.zero[:], 0.0).then_inc(S.z, 1)
+    ve.wait_ge(S.z, 1)
+    if client:
+        ve_own()
+    if r < last:
+        ve_serve()
+    if not client:
+        ve_own()
+
+    if client:
+        sc.wait_ge(S.on, o_eng(r - 1)[1])
+        sc.dma_start(T.y[:], T.yd[:]).then_inc(S.st, 16)
+    else:
+        sc.wait_ge(S.ydone, 1)
+        sc.dma_start(T.y[:], T.y_sb[:]).then_inc(S.st, 16)
     sc.wait_ge(S.st, 16)

from concourse.mybir import AluOpType

P, QP, BW, KB = 128, 64, 128, 4
ENG = 8
ENG_HEAD = 16

SCRATCH = {
    "qd":    ("dram", [P, QP], "bfloat16"),
    "yd":    ("dram", [P, QP], "bfloat16"),
    "q_sb":  ("sbuf", [P, QP], "bfloat16"),
    "qn_sb": ("sbuf", [P, QP], "bfloat16"),
    "k_sb":  ("sbuf", [P, KB * BW], "bfloat16"),
    "v_sb":  ("sbuf", [P, KB * BW], "bfloat16"),
    "kvx":   ("sbuf", [P, 2 * BW], "bfloat16"),
    "zero":  ("sbuf", [P, (KB + 1) * QP], "bfloat16"),
    "sn_sb": ("sbuf", [P, KB * QP], "bfloat16"),
    "so_sb": ("sbuf", [P, (KB + 1) * QP], "bfloat16"),
    "os_sb": ("sbuf", [P, QP], "bfloat16"),
    "on_sb": ("sbuf", [P, QP], "bfloat16"),
    "ps_sb": ("sbuf", [P, QP], "bfloat16"),
    "pn_sb": ("sbuf", [P, QP], "bfloat16"),
    "y_sb":  ("sbuf", [P, QP], "bfloat16"),
    "psn0":  ("psum", [P, 512], "float32"),
    "psn1":  ("psum", [P, 512], "float32"),
    "psn2":  ("psum", [P, 512], "float32"),
    "psn3":  ("psum", [P, 512], "float32"),
    "pon":   ("psum", [P, 512], "float32"),
    "pso":   ("psum", [P, 512], "float32"),
    "poo":   ("psum", [P, 512], "float32"),
}
SEMAPHORES = ["qd", "q", "k", "v", "kx", "z", "qn", "on", "kvn", "loc", "pn", "pc",
              "m1n0", "m1n1", "m1n2", "m1n3", "rn0", "rn1", "rn2", "rn3", "m2n", "cn",
              "m1o", "ro", "m2o", "ydone", "st"]


def _engines(topo, src, dst, want):
    full, m, cnt, bit = topo.mask(src, dst), 0, 0, 1
    while cnt < want and bit <= full:
        if full & bit:
            m |= bit
            cnt += 1
        bit <<= 1
    return m, cnt


def rank_program(g, core, T, topo):
    r = T.rank_of(core)
    if r is None:
        return
    cores, S = T.cores, T.sem
    last = len(cores) - 1
    te, ve, sy, sc = g.tensor, g.vector, g.sync, g.scalar
    head, second = (r == 0), (r == 1)

    def apart(i):
        a, b = cores[i - 1], cores[i]
        return (topo.host(a), topo.chip(a)) != (topo.host(b), topo.chip(b))

    client = r > 0 and apart(r)
    finisher = r < last and apart(r + 1)

    def q_eng(i):
        return _engines(topo, cores[i], cores[i - 1], ENG)

    def o_eng(i):
        return _engines(topo, cores[i], cores[i + 1], ENG_HEAD if i == 0 else ENG)

    def blk(t, b):
        return t[:, b * BW:(b + 1) * BW]

    if head:
        sy.dma_start(T.kvx[:, 0:BW], blk(T.k, KB - 1)).then_inc(S.kx, 16)
        sy.dma_start(T.kvx[:, BW:2 * BW], blk(T.v, KB - 1)).then_inc(S.kx, 16)
        w = (KB - 1) * BW
        sy.dma_start(T.k_sb[:, 0:w], T.k[:, 0:w]).then_inc(S.k, 16)
        sy.dma_start(T.v_sb[:, 0:w], T.v[:, 0:w]).then_inc(S.v, 16)
        sy.dma_start(T.q_sb[:], T.q[:]).then_inc(S.q, 16)
    else:
        sy.dma_start(T.qd[:], T.q[:]).then_inc(S.qd, 16)
        if client:
            sy.dma_start(T.q_sb[:], T.q[:]).then_inc(S.q, 16)
        sy.dma_start(T.k_sb[:], T.k[:]).then_inc(S.k, 16)
        sy.dma_start(T.v_sb[:], T.v[:]).then_inc(S.v, 16)
        if not client:
            sy.dma_start(T.q_sb[:], T.q[:]).then_inc(S.q, 16)

    kept = KB - 1 if head else KB
    nb = [(blk(T.k_sb, b), blk(T.v_sb, b)) for b in range(kept)]
    ob = list(nb)
    if head or second:
        ob.append((T.kvx[:, 0:BW], T.kvx[:, BW:2 * BW]))

    sent = 0
    if head:
        m, e = o_eng(0)
        rid, pid = topo.addr(cores[1], core)
        g.wait_ge(S.kx, 32)
        g.remote_dma(T.kvx[:], T.kvx[:], S.kvn, S.loc, pid, rid, m)
        sent += e
    else:
        m, e = q_eng(r)
        rid, pid = topo.addr(cores[r - 1], core)
        g.wait_ge(S.qd, 16)
        g.remote_dma(T.qn_sb[:], T.qd[:], S.qn, S.loc, pid, rid, m)
        sent += e
        if client:
            g.wait_ge(S.pc, 1)
            g.remote_dma(T.pn_sb[:], T.ps_sb[:], S.pn, S.loc, pid, rid, m)
            sent += e
    if r < last:
        m, e = o_eng(r)
        rid, pid = topo.addr(cores[r + 1], core)
        g.wait_ge(S.cn, 1)
        g.remote_dma(T.yd[:] if finisher else T.on_sb[:], T.os_sb[:], S.on, S.loc, pid, rid, m)
        sent += e
    g.wait_ge(S.loc, sent)

    def te_serve():
        te.wait_ge(S.k, 16)
        te.wait_ge(S.qn, q_eng(r + 1)[1])
        for i, (kb, vb) in enumerate(nb):
            te.matmul(T["psn%d" % i][:, 0:QP], kb, T.qn_sb[:], start=True, stop=True).then_inc(S["m1n%d" % i], 1)
        te.wait_ge(S.v, 16)
        for i, (kb, vb) in enumerate(nb):
            te.wait_ge(S["rn%d" % i], 1)
            te.matmul(T.pon[:, 0:QP], vb, T.sn_sb[:, i * QP:(i + 1) * QP],
                      start=(i == 0), stop=(i == len(nb) - 1)).then_inc(S.m2n, 1)

    def te_own():
        te.wait_ge(S.k, 16)
        te.wait_ge(S.q, 16)
        if head:
            te.wait_ge(S.kx, 32)
        if second:
            te.wait_ge(S.kvn, o_eng(0)[1])
        for i, (kb, vb) in enumerate(ob):
            te.matmul(T.pso[:, i * QP:(i + 1) * QP], kb, T.q_sb[:], start=True, stop=True).then_inc(S.m1o, 1)
        te.wait_ge(S.v, 16)
        te.wait_ge(S.ro, 1)
        for i, (kb, vb) in enumerate(ob):
            te.matmul(T.poo[:, 0:QP], vb, T.so_sb[:, i * QP:(i + 1) * QP],
                      start=(i == 0), stop=(i == len(ob) - 1)).then_inc(S.m2o, 1)

    if client:
        te_own()
    if r < last:
        te_serve()
    if not client:
        te_own()

    def ve_serve():
        for i in range(len(nb)):
            ve.wait_ge(S["m1n%d" % i], 1)
            ve.tensor_tensor(T.sn_sb[:, i * QP:(i + 1) * QP], T["psn%d" % i][:, 0:QP], T.zero[:, 0:QP],
                             AluOpType.max).then_inc(S["rn%d" % i], 1)
        ve.wait_ge(S.m2n, len(nb))
        if finisher:
            ve.wait_ge(S.pn, q_eng(r + 1)[1])
            ve.tensor_tensor(T.os_sb[:], T.pon[:, 0:QP], T.pn_sb[:], AluOpType.add).then_inc(S.cn, 1)
        else:
            ve.tensor_copy(T.os_sb[:], T.pon[:, 0:QP]).then_inc(S.cn, 1)

    def ve_own():
        wo = len(ob) * QP
        ve.wait_ge(S.m1o, len(ob))
        ve.tensor_tensor(T.so_sb[:, 0:wo], T.pso[:, 0:wo], T.zero[:, 0:wo], AluOpType.max).then_inc(S.ro, 1)
        ve.wait_ge(S.m2o, len(ob))
        if client:
            ve.tensor_copy(T.ps_sb[:], T.poo[:, 0:QP]).then_inc(S.pc, 1)
        elif head:
            ve.tensor_copy(T.y_sb[:], T.poo[:, 0:QP]).then_inc(S.ydone, 1)
        else:
            ve.wait_ge(S.on, o_eng(r - 1)[1])
            ve.tensor_tensor(T.y_sb[:], T.poo[:, 0:QP], T.on_sb[:], AluOpType.add).then_inc(S.ydone, 1)

    ve.memset(T.zero[:], 0.0).then_inc(S.z, 1)
    ve.wait_ge(S.z, 1)
    if client:
        ve_own()
    if r < last:
        ve_serve()
    if not client:
        ve_own()

    if client:
        sc.wait_ge(S.on, o_eng(r - 1)[1])
        sc.dma_start(T.y[:], T.yd[:]).then_inc(S.st, 16)
    else:
        sc.wait_ge(S.ydone, 1)
        sc.dma_start(T.y[:], T.y_sb[:]).then_inc(S.st, 16)
    sc.wait_ge(S.st, 16)
